import numpy as np
import ml_dtypes


def mxq(x, axis, fmt="e4m3"):
    dtype, down = {"e4m3": (ml_dtypes.float8_e4m3fn, 7), "e5m2": (ml_dtypes.float8_e5m2, 14)}[fmt]
    v = np.moveaxis(np.asarray(x, np.float32).astype(ml_dtypes.bfloat16).astype(np.float64), axis, -1)
    blocks = v.reshape(v.shape[:-1] + (-1, 32))
    amax = np.abs(blocks).max(-1, keepdims=True)
    byte = np.maximum(np.where(amax > 0, np.frexp(amax)[1] - 1 + 127, 0) - down, 1)
    scale = np.exp2(byte - 127.0)
    codes = (blocks / scale).astype(np.float32).astype(dtype).astype(np.float64)
    return np.moveaxis((codes * scale).reshape(v.shape), -1, axis)


WIDE = False


def mx_kscale(k):
    if not WIDE:
        return np.ones(k)
    levels = np.array([10, -10, 5, -5, 0])
    if k % 512:
        return np.exp2(np.random.permutation(np.resize(levels, k // 32))).repeat(32)
    a = np.empty((k // 512, 16))
    for p in range(k // 512):
        a[p, :8] = np.random.permutation(np.resize(levels, 8))
        for g in range(8):
            far = levels[np.abs(levels - a[p, g]) >= 10]
            a[p, g + 8] = far[np.random.randint(len(far))]
    return np.exp2(a.ravel()).repeat(32)


def f64(x):
    return np.asarray(x).astype(np.float64)


def striped(idx):
    return np.tile(idx.reshape(-1, 16).T, (8, 1)).astype(np.uint16)


def unstriped(offs):
    return offs[:16].T.reshape(-1).astype(np.int64)


E2M1 = np.array([0.0, 0.5, 1.0, 1.5, 2.0, 3.0, 4.0, 6.0, -0.0, -0.5, -1.0, -1.5, -2.0, -3.0, -4.0, -6.0])


def pack_weight(w, fmt):
    k, n = w.shape
    w = f64(np.asarray(w, np.float32).astype(ml_dtypes.bfloat16)).reshape(k // 32, 32, n)
    amax = np.abs(w).max(1)
    if fmt == "e4m3":
        byte = np.frexp(amax)[1] - 1 + 127 - 7
    else:
        mant, ex = np.frexp(amax / 6.0)
        byte = np.where(mant > 0.5, ex, ex - 1) + 127
    byte = np.clip(np.where(amax > 0, byte, 1), 1, 254)
    scaled = (w * np.exp2(127.0 - byte)[:, None, :]).reshape(k, n).astype(np.float32)
    by_word = np.ascontiguousarray(scaled.reshape(k // 512, 128, 4, n).transpose(0, 1, 3, 2))
    if fmt == "e4m3":
        words = by_word.astype(ml_dtypes.float8_e4m3fn).view(np.uint8)
    else:
        c = by_word.astype(ml_dtypes.float4_e2m1fn).view(np.uint8) & 0xF
        words = (c[..., 0::2] | (c[..., 1::2] << 4)).reshape(k // 512, 128, 2 * n)
    return np.ascontiguousarray(words), np.ascontiguousarray(byte.astype(np.uint8).reshape(k // 512, 16, n))


def unpack_weight(words, scales, fmt):
    g, _, n = scales.shape
    words = np.ascontiguousarray(words).reshape(g, 128, n, -1)
    if fmt == "e4m3":
        vals = words.view(ml_dtypes.float8_e4m3fn).astype(np.float64)
    else:
        nib = np.empty((g, 128, n, 4), np.uint8)
        nib[..., 0::2] = words & 0xF
        nib[..., 1::2] = words >> 4
        vals = E2M1[nib]
    vals = vals * np.repeat(np.exp2(scales.astype(np.float64) - 127.0), 8, axis=1)[..., None]
    return vals.transpose(0, 1, 3, 2).reshape(g * 512, n)


def gelu(v):
    return 0.5 * v * (1.0 + np.tanh(np.sqrt(2.0 / np.pi) * (v + 0.044715 * v**3)))


K, H, N, T, S, P = 512, 1536, 256, 4096, 1024, 512

def setup_inputs():
    n = np.random.standard_normal
    s = mx_kscale(K)[:, None]
    u = mx_kscale(H)[:, None]
    d = {}
    d["tab_words"], d["tab_scales"] = pack_weight(n((K, T)) * s, "e2m1")
    d["offs"] = striped(np.random.permutation(T)[:S])
    d["pos1"] = striped(np.random.permutation(S)[:P])
    d["pos2"] = striped(np.random.permutation(S)[:P])
    d["wg"] = (n((K, H)) / s * u.T / K**0.5).astype(np.float32)
    d["ww_words"], d["ww_scales"] = pack_weight(n((K, H)) / s * u.T / K**0.5, "e4m3")
    d["w3"] = (1.6 * n((H, N)) / u / H**0.5).astype(np.float32)
    d["b3"] = (0.7 * n(N)).astype(np.float32)
    d["w4_words"], d["w4_scales"] = pack_weight(0.9 * n((H, N)) / u / H**0.5, "e2m1")
    return d

def reference(tab_words, tab_scales, offs, pos1, pos2, wg, ww_words, ww_scales, w3, b3, w4_words, w4_scales):
    v = unpack_weight(tab_words, tab_scales, "e2m1")[:, unstriped(offs)]
    ww = unpack_weight(ww_words, ww_scales, "e4m3")
    w4 = unpack_weight(w4_words, w4_scales, "e2m1")
    give = mxq(f64(wg), 0, "e4m3").T @ v
    want = ww.T @ v
    z = np.maximum(give[:, unstriped(pos1)], want[:, unstriped(pos2)])
    zq = mxq(z, 0, "e4m3")
    y3 = (mxq(f64(w3), 0, "e4m3").T @ zq) + f64(b3)[:, None]
    y4 = w4.T @ zq
    return y3 / (1.0 + np.exp(-y3)) + y4

@@ -1,0 +1,252 @@
+from contextlib import ExitStack
+
+import concourse.mybir as mybir
+
+K, H, N, T, S, M = 512, 1536, 256, 4096, 1024, 512
+FLOPS = 2 * (2 * K * H * S + 2 * H * N * M)
+
+F32 = mybir.dt.float32
+BF16 = mybir.dt.bfloat16
+I32 = mybir.dt.int32
+U32 = mybir.dt.uint32
+U16 = mybir.dt.uint16
+U8 = mybir.dt.uint8
+E4M3 = mybir.dt.float8_e4m3fn_x4
+E2M1 = mybir.dt.float4_e2m1fn_x4
+
+P = 128
+PACK = 4
+PASS = P * PACK
+BANK = 512
+BLOCKS = H // PASS
+HALF = PASS // 2
+BANKS = 8
+IDLE = P - 16
+
+
+def load_scale_rows(nc, plane, rows):
+    for q in range(4):
+        nc.sync.dma_start(out=plane[32 * q : 32 * q + 4].bitcast(I32), in_=rows[4 * q : 4 * q + 4].bitcast(I32))
+
+
+def tile_list_first_message_ranker_kernel(
+    tc, tab_words, tab_scales, offs, pos1, pos2, wg, ww_words, ww_scales, w3, b3, w4_words, w4_scales, out
+):
+    nc = tc.nc
+    with ExitStack() as ctx:
+        held = ctx.enter_context(tc.tile_pool(name="held", bufs=1))
+        stage = ctx.enter_context(tc.tile_pool(name="stage", bufs=2))
+        rows = ctx.enter_context(tc.tile_pool(name="rows", bufs=1))
+        picked = ctx.enter_context(tc.tile_pool(name="picked", bufs=1))
+        psum = ctx.enter_context(tc.psum_pool(name="psum", bufs=1))
+
+        picks = held.tile([P, S // 16], U16, name="picks")
+        senders = held.tile([P, M // 16], U16, name="senders")
+        receivers = held.tile([P, M // 16], U16, name="receivers")
+        table_words = held.tile([P, T], U16, name="table_words")
+        table_scales = held.tile([P, T], U8, name="table_scales")
+        ww_scales_raw = held.tile([P, H], U8, name="ww_scales_raw")
+        w4_scale = held.tile([P, BLOCKS, N], U8, name="w4_scale", align_bytes=64)
+        w4_codes = held.tile([P, BLOCKS, 2 * N], U8, name="w4_codes", align_bytes=64)
+        bias = held.tile([P, N // P], F32, name="bias")
+        banks = [psum.tile([P, BANK], F32, name=f"bank{i}") for i in range(BANKS)]
+
+        v_scale = held.tile([P, S], U8, name="v_scale", align_bytes=64)
+        nc.vector.memset(table_scales[0:IDLE].bitcast(I32), 0)
+        nc.vector.memset(v_scale[:].bitcast(I32), 0)
+        nc.vector.memset(ww_scales_raw[:].bitcast(I32), 0)
+        nc.vector.memset(w4_scale[:].rearrange("p a n -> p (a n)").bitcast(I32), 0)
+
+        def load_wg(b, half):
+            raw = stage.tile([P, PACK, HALF], F32, name="raw")
+            c0 = PASS * b + HALF * half
+            nc.sync.dma_start(out=raw[:], in_=wg[:, c0 : c0 + HALF].rearrange("(p j) c -> p j c", j=PACK))
+            return raw
+
+        def weave_wg(raw, half, woven):
+            m0 = half * (P // 2)
+            nc.scalar.copy(
+                out=woven[:].rearrange("p (t m j) -> p m j t", t=PACK, j=PACK)[:, m0 : m0 + P // 2],
+                in_=raw[:].rearrange("p j (m t) -> p m j t", t=PACK),
+            )
+
+        def load_ww(b):
+            raw = held.tile([P, PASS], I32, name=f"ww_raw{b}")
+            words = ww_words[0].rearrange("p c i -> p (c i)")[:, PACK * PASS * b : PACK * PASS * (b + 1)]
+            nc.sync.dma_start(out=raw[:], in_=words.bitcast(I32))
+            return raw
+
+        def deal_ww(b, raw):
+            codes = held.tile([P, PASS], I32, name=f"ww_codes{b}", align_bytes=64)
+            scale = held.tile([P, PASS], U8, name=f"ww_scale{b}", align_bytes=64)
+            nc.vector.tensor_copy(
+                out=codes[:].rearrange("p (t m) -> p m t", t=PACK), in_=raw[:].rearrange("p (m t) -> p m t", t=PACK)
+            )
+            nc.vector.tensor_copy(
+                out=scale[:].rearrange("p (t m) -> p t m", t=PACK),
+                in_=ww_scales_raw[:, PASS * b : PASS * (b + 1)].rearrange("p (m t) -> p t m", t=PACK),
+            )
+            return codes, scale
+
+        def quantise(name, woven, width, on_row=None):
+            if on_row is None:
+                codes = held.tile([P, width], U32, name=f"{name}_codes", align_bytes=64)
+            else:
+                codes = rows.tile([P, width], U32, name=f"{name}_codes", tag=f"row{on_row}", align_bytes=64)
+            scale = held.tile([P, width], U8, name=f"{name}_scale", align_bytes=64)
+            nc.vector.quantize_mx(out=codes[:].bitcast(E4M3), scales=scale[:], in_=woven[:])
+            return codes, scale
+
+        nc.sync.dma_start(picks[:], offs)
+        nc.sync.dma_start(out=table_scales[IDLE:P].bitcast(I32), in_=tab_scales[0].bitcast(I32))
+        nc.sync.dma_start(out=table_words[:].bitcast(I32), in_=tab_words[0].bitcast(I32))
+        load_scale_rows(nc, ww_scales_raw, ww_scales[0])
+        ww_raw = [load_ww(0)]
+        wg_raw = [load_wg(0, 0)]
+        v_scale_rows = held.tile([P, S], U8, name="v_scale_rows")
+        nc.vector.tensor_copy(v_scale_rows[:], table_scales[:].indirect(picks[:]))
+        load_scale_rows(nc, v_scale, v_scale_rows[IDLE:P])
+        wg_raw.append(load_wg(0, 1))
+        ww_raw.extend(load_ww(b) for b in range(1, BLOCKS))
+        nc.sync.dma_start(receivers[:], pos2)
+        nc.sync.dma_start(senders[:], pos1)
+        nc.sync.dma_start(out=w4_codes[:].bitcast(I32), in_=w4_words.rearrange("a p w -> p a w").bitcast(I32))
+        load_scale_rows(nc, w4_scale, w4_scales.rearrange("a q n -> q a n"))
+        with nc.allow_non_contiguous_dma(reason="one bias value a partition"):
+            nc.sync.dma_start(out=bias[:], in_=b3.rearrange("(g p) -> p g", p=P))
+
+        v_words = [held.tile([P, BANK], U16, name=f"v_words{h}", align_bytes=64) for h in range(S // BANK)]
+        cols = BANK // 16
+        nc.vector.tensor_copy(v_words[0][:], table_words[:].indirect(picks[:, 0:cols]))
+        ww_q = [deal_ww(0, ww_raw[0])]
+        nc.vector.tensor_copy(v_words[1][:], table_words[:].indirect(picks[:, cols : 2 * cols]))
+
+        turn = [0]
+
+        def first_stage(weights, t, places, into):
+            codes, scale = weights
+            row = rows.tile([P, S], F32, name="row", tag=f"row{turn[0]}", align_bytes=64)
+            for h in range(S // BANK):
+                bank = banks[(2 * turn[0] + h) % BANKS]
+                nc.tensor.matmul_mx(
+                    out=bank[:],
+                    lhsT=codes[:, P * t : P * (t + 1)].bitcast(E4M3),
+                    lhsT_scale=scale[:, P * t : P * (t + 1)],
+                    rhs=v_words[h][:].bitcast(E2M1),
+                    rhs_scale=v_scale[:, BANK * h : BANK * (h + 1)],
+                    start=True,
+                    stop=True,
+                )
+                nc.scalar.copy(out=row[:, BANK * h : BANK * (h + 1)], in_=bank[:])
+            turn[0] = turn[0] + 1
+            span = M // 16 // len(into)
+            for u, piece in enumerate(into):
+                nc.vector.tensor_copy(piece[:, t, :], row[:].indirect(places[:, span * u : span * (u + 1)]))
+
+        def meet(z, given, wanted):
+            nc.vector.tensor_tensor(
+                out=z[:].rearrange("p (c i t) -> p c t i", i=2, t=PACK),
+                in0=given[:].rearrange("p t (c i) -> p c t i", i=2),
+                in1=wanted[:].rearrange("p t (c i) -> p c t i", i=2),
+                op=mybir.AluOpType.max,
+            )
+
+        def weave_w3(a):
+            raw = stage.tile([P, PACK, N], F32, name="raw")
+            nc.sync.dma_start(out=raw[:], in_=w3[PASS * a : PASS * (a + 1), :].rearrange("(p j) n -> p j n", j=PACK))
+            woven = stage.tile([P, PACK * N], BF16, name="w3_woven", align_bytes=64)
+            nc.scalar.copy(
+                out=woven[:].rearrange("p (c i j) -> p c j i", i=2, j=PACK),
+                in_=raw[:].rearrange("p j (c i) -> p c j i", i=2),
+            )
+            return woven
+
+        z_q, w3_q = [], []
+        woven = stage.tile([P, PACK * PASS], BF16, name="wg_woven", align_bytes=64)
+        for half in range(2):
+            weave_wg(wg_raw[half], half, woven)
+        wg_q = quantise("wg0", woven, PASS)
+        ww_q.extend(deal_ww(c, ww_raw[c]) for c in range(1, BLOCKS))
+        for b in range(BLOCKS):
+            pieces = 2 if b == BLOCKS - 1 else 1
+            before = (given, wanted) if b > 0 else None
+            wanted = [picked.tile([P, PACK, M // pieces], F32, name=f"wanted{b}_{u}") for u in range(pieces)]
+            given = [picked.tile([P, PACK, M // pieces], F32, name=f"given{b}_{u}") for u in range(pieces)]
+            first_stage(ww_q[b], 0, receivers, wanted)
+            if b > 0:
+                z = rows.tile([P, PACK * M], BF16, name="z", tag=f"row{turn[0] - 1}", align_bytes=64)
+                meet(z, before[0][0], before[1][0])
+                woven = stage.tile([P, PACK * PASS], BF16, name="wg_woven", align_bytes=64)
+                weave_wg(load_wg(b, 0), 0, woven)
+            first_stage(ww_q[b], 1, receivers, wanted)
+            if b > 0:
+                z_q.append(quantise(f"z{b - 1}", z, M, on_row=turn[0] - 1))
+                weave_wg(load_wg(b, 1), 1, woven)
+                wg_q = quantise(f"wg{b}", woven, PASS)
+            first_stage(ww_q[b], 2, receivers, wanted)
+            first_stage(ww_q[b], 3, receivers, wanted)
+            if b > 0:
+                w3_q.append(quantise(f"w3{b - 1}", weave_w3(b - 1), N))
+            for t in range(PACK):
+                first_stage(wg_q, t, senders, given)
+
+        WIDE = M // 2
+
+        def second_stage(a, u, z_codes, z_scale):
+            for g in range(N // P):
+                nc.tensor.matmul_mx(
+                    out=banks[4 * u + 2 * g][:, 0:WIDE],
+                    lhsT=w3_q[a][0][:, P * g : P * (g + 1)].bitcast(E4M3),
+                    lhsT_scale=w3_q[a][1][:, P * g : P * (g + 1)],
+                    rhs=z_codes.bitcast(E4M3),
+                    rhs_scale=z_scale,
+                    start=(a == 0),
+                    stop=(a == BLOCKS - 1),
+                )
+                for c in range(WIDE // P):
+                    nc.tensor.matmul_mx(
+                        out=banks[4 * u + 2 * g + 1][:, P * c : P * (c + 1)],
+                        lhsT=w4_codes[:, a, 2 * P * g : 2 * P * (g + 1)].bitcast(E2M1),
+                        lhsT_scale=w4_scale[:, a, P * g : P * (g + 1)],
+                        rhs=z_codes[:, P * c : P * (c + 1)].bitcast(E4M3),
+                        rhs_scale=z_scale[:, P * c : P * (c + 1)],
+                        start=(a == 0 and c == 0),
+                        stop=(a == BLOCKS - 1 and c == WIDE // P - 1),
+                    )
+
+        def gate(u, g):
+            gated = picked.tile([P, WIDE], F32, name=f"gated{u}_{g}")
+            nc.scalar.activation(
+                out=gated[:],
+                in_=banks[4 * u + 2 * g][:, 0:WIDE],
+                func=mybir.ActivationFunctionType.Silu,
+                bias=bias[:, g : g + 1],
+            )
+            return gated
+
+        def finish(u, g, gated):
+            score = picked.tile([P, WIDE], F32, name=f"score{u}_{g}")
+            nc.vector.tensor_tensor(
+                out=score[:], in0=banks[4 * u + 2 * g + 1][:, 0:WIDE], in1=gated[:], op=mybir.AluOpType.add
+            )
+            nc.sync.dma_start(out=out[P * g : P * (g + 1), WIDE * u : WIDE * (u + 1)], in_=score[:])
+
+        for a in range(BLOCKS - 1):
+            for u in range(2):
+                cut = slice(WIDE * u, WIDE * (u + 1))
+                second_stage(a, u, z_q[a][0][:, cut], z_q[a][1][:, cut])
+        last = BLOCKS - 1
+        woven = weave_w3(last)
+        z_last = [picked.tile([P, PACK * WIDE], BF16, name=f"z_last{u}", align_bytes=64) for u in range(2)]
+        meet(z_last[0], given[0], wanted[0])
+        w3_q.append(quantise(f"w3{last}", woven, N))
+        codes, scale = quantise("z_last0", z_last[0], WIDE)
+        second_stage(last, 0, codes[:], scale[:])
+        gated = [gate(0, g) for g in range(N // P)]
+        meet(z_last[1], given[1], wanted[1])
+        finish(0, 0, gated[0])
+        codes, scale = quantise("z_last1", z_last[1], WIDE)
+        second_stage(last, 1, codes[:], scale[:])
+        finish(0, 1, gated[1])
+        for g in range(N // P):
+            finish(1, g, gate(1, g))

@@ -24,9 +24,9 @@ BANKS = 8
 IDLE = P - 16
 
 
-def load_scale_rows(nc, plane, rows):
+def load_scale_rows(queue, plane, rows):
     for q in range(4):
-        nc.sync.dma_start(out=plane[32 * q : 32 * q + 4].bitcast(I32), in_=rows[4 * q : 4 * q + 4].bitcast(I32))
+        queue.dma_start(out=plane[32 * q : 32 * q + 4].bitcast(I32), in_=rows[4 * q : 4 * q + 4].bitcast(I32))
 
 
 def tile_list_first_message_ranker_kernel(
@@ -58,7 +58,10 @@ def tile_list_first_message_ranker_kernel(
         nc.vector.memset(w4_scale[:].rearrange("p a n -> p (a n)").bitcast(I32), 0)
 
         def load_wg(b, half):
-            raw = stage.tile([P, PACK, HALF], F32, name="raw")
+            if b == 0:
+                raw = rows.tile([P, PACK, HALF], F32, name="raw0", tag=f"row{1 - half}", align_bytes=64)
+            else:
+                raw = stage.tile([P, PACK, HALF], F32, name="raw")
             c0 = PASS * b + HALF * half
             nc.sync.dma_start(out=raw[:], in_=wg[:, c0 : c0 + HALF].rearrange("(p j) c -> p j c", j=PACK))
             return raw
@@ -70,23 +73,27 @@ def tile_list_first_message_ranker_kernel(
                 in_=raw[:].rearrange("p j (m t) -> p m j t", t=PACK),
             )
 
-        def load_ww(b):
-            raw = held.tile([P, PASS], I32, name=f"ww_raw{b}")
-            words = ww_words[0].rearrange("p c i -> p (c i)")[:, PACK * PASS * b : PACK * PASS * (b + 1)]
+        def load_ww(b0, b1):
+            raw = picked.tile([P, PASS * (b1 - b0)], I32, name=f"ww_raw{b0}", tag=f"ww_raw{b0}", align_bytes=64)
+            words = ww_words[0].rearrange("p c i -> p (c i)")[:, PACK * PASS * b0 : PACK * PASS * b1]
             nc.sync.dma_start(out=raw[:], in_=words.bitcast(I32))
             return raw
 
-        def deal_ww(b, raw):
-            codes = held.tile([P, PASS], I32, name=f"ww_codes{b}", align_bytes=64)
-            scale = held.tile([P, PASS], U8, name=f"ww_scale{b}", align_bytes=64)
+        def deal_ww(b0, b1, raw, scale_tag):
+            width = PASS * (b1 - b0)
+            codes = held.tile([P, width], I32, name=f"ww_codes{b0}", align_bytes=64)
+            scale = picked.tile([P, width], U8, name=f"ww_scale{b0}", tag=scale_tag, align_bytes=64)
             nc.vector.tensor_copy(
-                out=codes[:].rearrange("p (t m) -> p m t", t=PACK), in_=raw[:].rearrange("p (m t) -> p m t", t=PACK)
+                out=codes[:].rearrange("p (b t m) -> p b m t", t=PACK, m=P),
+                in_=raw[:].rearrange("p (b m t) -> p b m t", t=PACK, m=P),
             )
             nc.vector.tensor_copy(
-                out=scale[:].rearrange("p (t m) -> p t m", t=PACK),
-                in_=ww_scales_raw[:, PASS * b : PASS * (b + 1)].rearrange("p (m t) -> p t m", t=PACK),
+                out=scale[:].rearrange("p (b t m) -> p b t m", t=PACK, m=P),
+                in_=ww_scales_raw[:, PASS * b0 : PASS * b1].rearrange("p (b m t) -> p b t m", t=PACK, m=P),
             )
-            return codes, scale
+            return [
+                (codes[:, PASS * b : PASS * (b + 1)], scale[:, PASS * b : PASS * (b + 1)]) for b in range(b1 - b0)
+            ]
 
         def quantise(name, woven, width, on_row=None):
             if on_row is None:
@@ -100,26 +107,23 @@ def tile_list_first_message_ranker_kernel(
         nc.sync.dma_start(picks[:], offs)
         nc.sync.dma_start(out=table_scales[IDLE:P].bitcast(I32), in_=tab_scales[0].bitcast(I32))
         nc.sync.dma_start(out=table_words[:].bitcast(I32), in_=tab_words[0].bitcast(I32))
-        load_scale_rows(nc, ww_scales_raw, ww_scales[0])
-        ww_raw = [load_ww(0)]
-        wg_raw = [load_wg(0, 0)]
+        load_scale_rows(nc.sync, ww_scales_raw, ww_scales[0])
+        ww_first = load_ww(0, 1)
+        wg_raw = [load_wg(0, half) for half in range(2)]
         v_scale_rows = held.tile([P, S], U8, name="v_scale_rows")
         nc.vector.tensor_copy(v_scale_rows[:], table_scales[:].indirect(picks[:]))
-        load_scale_rows(nc, v_scale, v_scale_rows[IDLE:P])
-        wg_raw.append(load_wg(0, 1))
-        ww_raw.extend(load_ww(b) for b in range(1, BLOCKS))
+        load_scale_rows(nc.sync, v_scale, v_scale_rows[IDLE:P])
+        ww_rest = load_ww(1, BLOCKS)
         nc.sync.dma_start(receivers[:], pos2)
         nc.sync.dma_start(senders[:], pos1)
         nc.sync.dma_start(out=w4_codes[:].bitcast(I32), in_=w4_words.rearrange("a p w -> p a w").bitcast(I32))
-        load_scale_rows(nc, w4_scale, w4_scales.rearrange("a q n -> q a n"))
+        load_scale_rows(nc.sync, w4_scale, w4_scales.rearrange("a q n -> q a n"))
         with nc.allow_non_contiguous_dma(reason="one bias value a partition"):
             nc.sync.dma_start(out=bias[:], in_=b3.rearrange("(g p) -> p g", p=P))
 
-        v_words = [held.tile([P, BANK], U16, name=f"v_words{h}", align_bytes=64) for h in range(S // BANK)]
-        cols = BANK // 16
-        nc.vector.tensor_copy(v_words[0][:], table_words[:].indirect(picks[:, 0:cols]))
-        ww_q = [deal_ww(0, ww_raw[0])]
-        nc.vector.tensor_copy(v_words[1][:], table_words[:].indirect(picks[:, cols : 2 * cols]))
+        v_words = held.tile([P, S], U16, name="v_words", align_bytes=64)
+        nc.vector.tensor_copy(v_words[:], table_words[:].indirect(picks[:]))
+        ww_q = deal_ww(0, 1, ww_first, "ww_scale0")
 
         turn = [0]
 
@@ -132,22 +136,20 @@ def tile_list_first_message_ranker_kernel(
                     out=bank[:],
                     lhsT=codes[:, P * t : P * (t + 1)].bitcast(E4M3),
                     lhsT_scale=scale[:, P * t : P * (t + 1)],
-                    rhs=v_words[h][:].bitcast(E2M1),
+                    rhs=v_words[:, BANK * h : BANK * (h + 1)].bitcast(E2M1),
                     rhs_scale=v_scale[:, BANK * h : BANK * (h + 1)],
                     start=True,
                     stop=True,
                 )
                 nc.scalar.copy(out=row[:, BANK * h : BANK * (h + 1)], in_=bank[:])
             turn[0] = turn[0] + 1
-            span = M // 16 // len(into)
-            for u, piece in enumerate(into):
-                nc.vector.tensor_copy(piece[:, t, :], row[:].indirect(places[:, span * u : span * (u + 1)]))
+            nc.vector.tensor_copy(into[:, t, :], row[:].indirect(places[:]))
 
         def meet(z, given, wanted):
             nc.vector.tensor_tensor(
                 out=z[:].rearrange("p (c i t) -> p c t i", i=2, t=PACK),
-                in0=given[:].rearrange("p t (c i) -> p c t i", i=2),
-                in1=wanted[:].rearrange("p t (c i) -> p c t i", i=2),
+                in0=given.rearrange("p t (c i) -> p c t i", i=2),
+                in1=wanted.rearrange("p t (c i) -> p c t i", i=2),
                 op=mybir.AluOpType.max,
             )
 
@@ -166,16 +168,16 @@ def tile_list_first_message_ranker_kernel(
         for half in range(2):
             weave_wg(wg_raw[half], half, woven)
         wg_q = quantise("wg0", woven, PASS)
-        ww_q.extend(deal_ww(c, ww_raw[c]) for c in range(1, BLOCKS))
+        ww_q.extend(deal_ww(1, BLOCKS, ww_rest, "ww_raw0"))
         for b in range(BLOCKS):
-            pieces = 2 if b == BLOCKS - 1 else 1
             before = (given, wanted) if b > 0 else None
-            wanted = [picked.tile([P, PACK, M // pieces], F32, name=f"wanted{b}_{u}") for u in range(pieces)]
-            given = [picked.tile([P, PACK, M // pieces], F32, name=f"given{b}_{u}") for u in range(pieces)]
+            tag = "ww_raw1" if b == 0 else f"wanted{b}"
+            wanted = picked.tile([P, PACK, M], F32, name=f"wanted{b}", tag=tag, align_bytes=64)
+            given = picked.tile([P, PACK, M], F32, name=f"given{b}")
             first_stage(ww_q[b], 0, receivers, wanted)
             if b > 0:
                 z = rows.tile([P, PACK * M], BF16, name="z", tag=f"row{turn[0] - 1}", align_bytes=64)
-                meet(z, before[0][0], before[1][0])
+                meet(z, before[0][:], before[1][:])
                 woven = stage.tile([P, PACK * PASS], BF16, name="wg_woven", align_bytes=64)
                 weave_wg(load_wg(b, 0), 0, woven)
             first_stage(ww_q[b], 1, receivers, wanted)
@@ -185,8 +187,10 @@ def tile_list_first_message_ranker_kernel(
                 wg_q = quantise(f"wg{b}", woven, PASS)
             first_stage(ww_q[b], 2, receivers, wanted)
             first_stage(ww_q[b], 3, receivers, wanted)
-            if b > 0:
-                w3_q.append(quantise(f"w3{b - 1}", weave_w3(b - 1), N))
+            if b == 1:
+                w3_q.append(quantise("w30", weave_w3(0), N))
+            if b == 2:
+                w3_woven = weave_w3(1)
             for t in range(PACK):
                 first_stage(wg_q, t, senders, given)
 
@@ -231,6 +235,7 @@ def tile_list_first_message_ranker_kernel(
             )
             nc.sync.dma_start(out=out[P * g : P * (g + 1), WIDE * u : WIDE * (u + 1)], in_=score[:])
 
+        w3_q.append(quantise("w31", w3_woven, N, on_row=turn[0] - 1))
         for a in range(BLOCKS - 1):
             for u in range(2):
                 cut = slice(WIDE * u, WIDE * (u + 1))
@@ -238,15 +243,13 @@ def tile_list_first_message_ranker_kernel(
         last = BLOCKS - 1
         woven = weave_w3(last)
         z_last = [picked.tile([P, PACK * WIDE], BF16, name=f"z_last{u}", align_bytes=64) for u in range(2)]
-        meet(z_last[0], given[0], wanted[0])
+        for u in range(2):
+            cut = slice(WIDE * u, WIDE * (u + 1))
+            meet(z_last[u], given[:, :, cut], wanted[:, :, cut])
         w3_q.append(quantise(f"w3{last}", woven, N))
-        codes, scale = quantise("z_last0", z_last[0], WIDE)
-        second_stage(last, 0, codes[:], scale[:])
-        gated = [gate(0, g) for g in range(N // P)]
-        meet(z_last[1], given[1], wanted[1])
-        finish(0, 0, gated[0])
-        codes, scale = quantise("z_last1", z_last[1], WIDE)
-        second_stage(last, 1, codes[:], scale[:])
-        finish(0, 1, gated[1])
-        for g in range(N // P):
-            finish(1, g, gate(1, g))
+        for u in range(2):
+            codes, scale = quantise(f"z_last{u}", z_last[u], WIDE)
+            second_stage(last, u, codes[:], scale[:])
+        for u in range(2):
+            for g in range(N // P):
+                finish(u, g, gate(u, g))

@@ -57,11 +57,11 @@ def tile_list_first_message_ranker_kernel(
         nc.vector.memset(ww_scales_raw[:].bitcast(I32), 0)
         nc.vector.memset(w4_scale[:].rearrange("p a n -> p (a n)").bitcast(I32), 0)
 
+        def raw_slot(b, half):
+            return f"spare{half}" if b == 1 else f"row{1 - half}"
+
         def load_wg(b, half):
-            if b == 0:
-                raw = rows.tile([P, PACK, HALF], F32, name="raw0", tag=f"row{1 - half}", align_bytes=64)
-            else:
-                raw = stage.tile([P, PACK, HALF], F32, name="raw")
+            raw = rows.tile([P, PACK, HALF], F32, name="wg_raw", tag=raw_slot(b, half), align_bytes=64)
             c0 = PASS * b + HALF * half
             nc.sync.dma_start(out=raw[:], in_=wg[:, c0 : c0 + HALF].rearrange("(p j) c -> p j c", j=PACK))
             return raw
@@ -95,11 +95,11 @@ def tile_list_first_message_ranker_kernel(
                 (codes[:, PASS * b : PASS * (b + 1)], scale[:, PASS * b : PASS * (b + 1)]) for b in range(b1 - b0)
             ]
 
-        def quantise(name, woven, width, on_row=None):
-            if on_row is None:
+        def quantise(name, woven, width, slot=None):
+            if slot is None:
                 codes = held.tile([P, width], U32, name=f"{name}_codes", align_bytes=64)
             else:
-                codes = rows.tile([P, width], U32, name=f"{name}_codes", tag=f"row{on_row}", align_bytes=64)
+                codes = rows.tile([P, width], U32, name=f"{name}_codes", tag=slot, align_bytes=64)
             scale = held.tile([P, width], U8, name=f"{name}_scale", align_bytes=64)
             nc.vector.quantize_mx(out=codes[:].bitcast(E4M3), scales=scale[:], in_=woven[:])
             return codes, scale
@@ -108,8 +108,8 @@ def tile_list_first_message_ranker_kernel(
         nc.sync.dma_start(out=table_scales[IDLE:P].bitcast(I32), in_=tab_scales[0].bitcast(I32))
         nc.sync.dma_start(out=table_words[:].bitcast(I32), in_=tab_words[0].bitcast(I32))
         load_scale_rows(nc.sync, ww_scales_raw, ww_scales[0])
-        ww_first = load_ww(0, 1)
         wg_raw = [load_wg(0, half) for half in range(2)]
+        ww_first = load_ww(0, 1)
         v_scale_rows = held.tile([P, S], U8, name="v_scale_rows")
         nc.vector.tensor_copy(v_scale_rows[:], table_scales[:].indirect(picks[:]))
         load_scale_rows(nc.sync, v_scale, v_scale_rows[IDLE:P])
@@ -147,19 +147,19 @@ def tile_list_first_message_ranker_kernel(
 
         def meet(z, given, wanted):
             nc.vector.tensor_tensor(
-                out=z[:].rearrange("p (c i t) -> p c t i", i=2, t=PACK),
-                in0=given.rearrange("p t (c i) -> p c t i", i=2),
-                in1=wanted.rearrange("p t (c i) -> p c t i", i=2),
+                out=z[:].rearrange("p (c i t) -> p c t i", i=PACK, t=PACK),
+                in0=given.rearrange("p t (c i) -> p c t i", i=PACK),
+                in1=wanted.rearrange("p t (c i) -> p c t i", i=PACK),
                 op=mybir.AluOpType.max,
             )
 
         def weave_w3(a):
-            raw = stage.tile([P, PACK, N], F32, name="raw")
+            raw = rows.tile([P, PACK, N], F32, name="w3_raw", tag=f"row{2 + a}", align_bytes=64)
             nc.sync.dma_start(out=raw[:], in_=w3[PASS * a : PASS * (a + 1), :].rearrange("(p j) n -> p j n", j=PACK))
-            woven = stage.tile([P, PACK * N], BF16, name="w3_woven", align_bytes=64)
+            woven = stage.tile([P, PACK * N], BF16, name="w3_woven", bufs=BLOCKS, align_bytes=64)
             nc.scalar.copy(
-                out=woven[:].rearrange("p (c i j) -> p c j i", i=2, j=PACK),
-                in_=raw[:].rearrange("p j (c i) -> p c j i", i=2),
+                out=woven[:].rearrange("p (c i j) -> p c j i", i=PACK, j=PACK),
+                in_=raw[:].rearrange("p j (c i) -> p c j i", i=PACK),
             )
             return woven
 
@@ -176,21 +176,17 @@ def tile_list_first_message_ranker_kernel(
             given = picked.tile([P, PACK, M], F32, name=f"given{b}")
             first_stage(ww_q[b], 0, receivers, wanted)
             if b > 0:
-                z = rows.tile([P, PACK * M], BF16, name="z", tag=f"row{turn[0] - 1}", align_bytes=64)
-                meet(z, before[0][:], before[1][:])
                 woven = stage.tile([P, PACK * PASS], BF16, name="wg_woven", align_bytes=64)
                 weave_wg(load_wg(b, 0), 0, woven)
+                z = rows.tile([P, PACK * M], BF16, name="z", tag=raw_slot(b, 0), align_bytes=64)
+                meet(z, before[0][:], before[1][:])
             first_stage(ww_q[b], 1, receivers, wanted)
             if b > 0:
-                z_q.append(quantise(f"z{b - 1}", z, M, on_row=turn[0] - 1))
                 weave_wg(load_wg(b, 1), 1, woven)
                 wg_q = quantise(f"wg{b}", woven, PASS)
+                z_q.append(quantise(f"z{b - 1}", z, M, slot=raw_slot(b, 1)))
             first_stage(ww_q[b], 2, receivers, wanted)
             first_stage(ww_q[b], 3, receivers, wanted)
-            if b == 1:
-                w3_q.append(quantise("w30", weave_w3(0), N))
-            if b == 2:
-                w3_woven = weave_w3(1)
             for t in range(PACK):
                 first_stage(wg_q, t, senders, given)
 
@@ -235,18 +231,18 @@ def tile_list_first_message_ranker_kernel(
             )
             nc.sync.dma_start(out=out[P * g : P * (g + 1), WIDE * u : WIDE * (u + 1)], in_=score[:])
 
-        w3_q.append(quantise("w31", w3_woven, N, on_row=turn[0] - 1))
-        for a in range(BLOCKS - 1):
-            for u in range(2):
-                cut = slice(WIDE * u, WIDE * (u + 1))
-                second_stage(a, u, z_q[a][0][:, cut], z_q[a][1][:, cut])
         last = BLOCKS - 1
-        woven = weave_w3(last)
-        z_last = [picked.tile([P, PACK * WIDE], BF16, name=f"z_last{u}", align_bytes=64) for u in range(2)]
-        for u in range(2):
-            cut = slice(WIDE * u, WIDE * (u + 1))
-            meet(z_last[u], given[:, :, cut], wanted[:, :, cut])
-        w3_q.append(quantise(f"w3{last}", woven, N))
+        z_last = []
+        for a in range(BLOCKS):
+            w3_q.append(quantise(f"w3{a}", weave_w3(a), N))
+            if a < last:
+                cut = slice(WIDE * a, WIDE * (a + 1))
+                z = rows.tile([P, PACK * WIDE], BF16, name="z_last", tag=f"row{2 + a}", align_bytes=64)
+                meet(z, given[:, :, cut], wanted[:, :, cut])
+                z_last.append(z)
+                for u in range(2):
+                    cut = slice(WIDE * u, WIDE * (u + 1))
+                    second_stage(a, u, z_q[a][0][:, cut], z_q[a][1][:, cut])
         for u in range(2):
             codes, scale = quantise(f"z_last{u}", z_last[u], WIDE)
             second_stage(last, u, codes[:], scale[:])

from contextlib import ExitStack

import concourse.mybir as mybir

K, H, N, T, S, M = 512, 1536, 256, 4096, 1024, 512
FLOPS = 2 * (2 * K * H * S + 2 * H * N * M)

F32 = mybir.dt.float32
BF16 = mybir.dt.bfloat16
I32 = mybir.dt.int32
U32 = mybir.dt.uint32
U16 = mybir.dt.uint16
U8 = mybir.dt.uint8
E4M3 = mybir.dt.float8_e4m3fn_x4
E2M1 = mybir.dt.float4_e2m1fn_x4

P = 128
PACK = 4
PASS = P * PACK
BANK = 512
BLOCKS = H // PASS
HALF = PASS // 2
BANKS = 8
IDLE = P - 16


def load_scale_rows(queue, plane, rows):
    for q in range(4):
        queue.dma_start(out=plane[32 * q : 32 * q + 4].bitcast(I32), in_=rows[4 * q : 4 * q + 4].bitcast(I32))


def tile_list_first_message_ranker_kernel(
    tc, tab_words, tab_scales, offs, pos1, pos2, wg, ww_words, ww_scales, w3, b3, w4_words, w4_scales, out
):
    nc = tc.nc
    with ExitStack() as ctx:
        held = ctx.enter_context(tc.tile_pool(name="held", bufs=1))
        stage = ctx.enter_context(tc.tile_pool(name="stage", bufs=2))
        rows = ctx.enter_context(tc.tile_pool(name="rows", bufs=1))
        picked = ctx.enter_context(tc.tile_pool(name="picked", bufs=1))
        psum = ctx.enter_context(tc.psum_pool(name="psum", bufs=1))

        picks = held.tile([P, S // 16], U16, name="picks")
        senders = held.tile([P, M // 16], U16, name="senders")
        receivers = held.tile([P, M // 16], U16, name="receivers")
        table_words = held.tile([P, T], U16, name="table_words")
        table_scales = held.tile([P, T], U8, name="table_scales")
        ww_scales_raw = held.tile([P, H], U8, name="ww_scales_raw")
        w4_scale = held.tile([P, BLOCKS, N], U8, name="w4_scale", align_bytes=64)
        w4_codes = held.tile([P, BLOCKS, 2 * N], U8, name="w4_codes", align_bytes=64)
        bias = held.tile([P, N // P], F32, name="bias")
        banks = [psum.tile([P, BANK], F32, name=f"bank{i}") for i in range(BANKS)]

        v_scale = held.tile([P, S], U8, name="v_scale", align_bytes=64)
        nc.vector.memset(table_scales[0:IDLE].bitcast(I32), 0)
        nc.vector.memset(v_scale[:].bitcast(I32), 0)
        nc.vector.memset(ww_scales_raw[:].bitcast(I32), 0)
        nc.vector.memset(w4_scale[:].rearrange("p a n -> p (a n)").bitcast(I32), 0)

        def raw_slot(b, half):
            return f"spare{half}" if b == 1 else f"row{1 - half}"

        def load_wg(b, half):
            raw = rows.tile([P, PACK, HALF], F32, name="wg_raw", tag=raw_slot(b, half), align_bytes=64)
            c0 = PASS * b + HALF * half
            nc.sync.dma_start(out=raw[:], in_=wg[:, c0 : c0 + HALF].rearrange("(p j) c -> p j c", j=PACK))
            return raw

        def weave_wg(raw, half, woven):
            m0 = half * (P // 2)
            nc.scalar.copy(
                out=woven[:].rearrange("p (t m j) -> p m j t", t=PACK, j=PACK)[:, m0 : m0 + P // 2],
                in_=raw[:].rearrange("p j (m t) -> p m j t", t=PACK),
            )

        def load_ww(b0, b1):
            raw = picked.tile([P, PASS * (b1 - b0)], I32, name=f"ww_raw{b0}", tag=f"ww_raw{b0}", align_bytes=64)
            words = ww_words[0].rearrange("p c i -> p (c i)")[:, PACK * PASS * b0 : PACK * PASS * b1]
            nc.sync.dma_start(out=raw[:], in_=words.bitcast(I32))
            return raw

        def deal_ww(b0, b1, raw, scale_tag):
            width = PASS * (b1 - b0)
            codes = held.tile([P, width], I32, name=f"ww_codes{b0}", align_bytes=64)
            scale = picked.tile([P, width], U8, name=f"ww_scale{b0}", tag=scale_tag, align_bytes=64)
            nc.vector.tensor_copy(
                out=codes[:].rearrange("p (b t m) -> p b m t", t=PACK, m=P),
                in_=raw[:].rearrange("p (b m t) -> p b m t", t=PACK, m=P),
            )
            nc.vector.tensor_copy(
                out=scale[:].rearrange("p (b t m) -> p b t m", t=PACK, m=P),
                in_=ww_scales_raw[:, PASS * b0 : PASS * b1].rearrange("p (b m t) -> p b t m", t=PACK, m=P),
            )
            return [
                (codes[:, PASS * b : PASS * (b + 1)], scale[:, PASS * b : PASS * (b + 1)]) for b in range(b1 - b0)
            ]

        def quantise(name, woven, width, slot=None):
            if slot is None:
                codes = held.tile([P, width], U32, name=f"{name}_codes", align_bytes=64)
            else:
                codes = rows.tile([P, width], U32, name=f"{name}_codes", tag=slot, align_bytes=64)
            scale = held.tile([P, width], U8, name=f"{name}_scale", align_bytes=64)
            nc.vector.quantize_mx(out=codes[:].bitcast(E4M3), scales=scale[:], in_=woven[:])
            return codes, scale

        nc.sync.dma_start(picks[:], offs)
        nc.sync.dma_start(out=table_scales[IDLE:P].bitcast(I32), in_=tab_scales[0].bitcast(I32))
        nc.sync.dma_start(out=table_words[:].bitcast(I32), in_=tab_words[0].bitcast(I32))
        load_scale_rows(nc.sync, ww_scales_raw, ww_scales[0])
        wg_raw = [load_wg(0, half) for half in range(2)]
        ww_first = load_ww(0, 1)
        v_scale_rows = held.tile([P, S], U8, name="v_scale_rows")
        nc.vector.tensor_copy(v_scale_rows[:], table_scales[:].indirect(picks[:]))
        load_scale_rows(nc.sync, v_scale, v_scale_rows[IDLE:P])
        ww_rest = load_ww(1, BLOCKS)
        nc.sync.dma_start(receivers[:], pos2)
        nc.sync.dma_start(senders[:], pos1)
        nc.sync.dma_start(out=w4_codes[:].bitcast(I32), in_=w4_words.rearrange("a p w -> p a w").bitcast(I32))
        load_scale_rows(nc.sync, w4_scale, w4_scales.rearrange("a q n -> q a n"))
        with nc.allow_non_contiguous_dma(reason="one bias value a partition"):
            nc.sync.dma_start(out=bias[:], in_=b3.rearrange("(g p) -> p g", p=P))

        v_words = held.tile([P, S], U16, name="v_words", align_bytes=64)
        nc.vector.tensor_copy(v_words[:], table_words[:].indirect(picks[:]))
        ww_q = deal_ww(0, 1, ww_first, "ww_scale0")

        turn = [0]

        def first_stage(weights, t, places, into):
            codes, scale = weights
            row = rows.tile([P, S], F32, name="row", tag=f"row{turn[0]}", align_bytes=64)
            for h in range(S // BANK):
                bank = banks[(2 * turn[0] + h) % BANKS]
                nc.tensor.matmul_mx(
                    out=bank[:],
                    lhsT=codes[:, P * t : P * (t + 1)].bitcast(E4M3),
                    lhsT_scale=scale[:, P * t : P * (t + 1)],
                    rhs=v_words[:, BANK * h : BANK * (h + 1)].bitcast(E2M1),
                    rhs_scale=v_scale[:, BANK * h : BANK * (h + 1)],
                    start=True,
                    stop=True,
                )
                nc.scalar.copy(out=row[:, BANK * h : BANK * (h + 1)], in_=bank[:])
            turn[0] = turn[0] + 1
            nc.vector.tensor_copy(into[:, t, :], row[:].indirect(places[:]))

        def meet(z, given, wanted):
            nc.vector.tensor_tensor(
                out=z[:].rearrange("p (c i t) -> p c t i", i=PACK, t=PACK),
                in0=given.rearrange("p t (c i) -> p c t i", i=PACK),
                in1=wanted.rearrange("p t (c i) -> p c t i", i=PACK),
                op=mybir.AluOpType.max,
            )

        def weave_w3(a):
            raw = rows.tile([P, PACK, N], F32, name="w3_raw", tag=f"row{2 + a}", align_bytes=64)
            nc.sync.dma_start(out=raw[:], in_=w3[PASS * a : PASS * (a + 1), :].rearrange("(p j) n -> p j n", j=PACK))
            woven = stage.tile([P, PACK * N], BF16, name="w3_woven", bufs=BLOCKS, align_bytes=64)
            nc.scalar.copy(
                out=woven[:].rearrange("p (c i j) -> p c j i", i=PACK, j=PACK),
                in_=raw[:].rearrange("p j (c i) -> p c j i", i=PACK),
            )
            return woven

        z_q, w3_q = [], []
        woven = stage.tile([P, PACK * PASS], BF16, name="wg_woven", align_bytes=64)
        for half in range(2):
            weave_wg(wg_raw[half], half, woven)
        wg_q = quantise("wg0", woven, PASS)
        ww_q.extend(deal_ww(1, BLOCKS, ww_rest, "ww_raw0"))
        for b in range(BLOCKS):
            before = (given, wanted) if b > 0 else None
            tag = "ww_raw1" if b == 0 else f"wanted{b}"
            wanted = picked.tile([P, PACK, M], F32, name=f"wanted{b}", tag=tag, align_bytes=64)
            given = picked.tile([P, PACK, M], F32, name=f"given{b}")
            first_stage(ww_q[b], 0, receivers, wanted)
            if b > 0:
                woven = stage.tile([P, PACK * PASS], BF16, name="wg_woven", align_bytes=64)
                weave_wg(load_wg(b, 0), 0, woven)
                z = rows.tile([P, PACK * M], BF16, name="z", tag=raw_slot(b, 0), align_bytes=64)
                meet(z, before[0][:], before[1][:])
            first_stage(ww_q[b], 1, receivers, wanted)
            if b > 0:
                weave_wg(load_wg(b, 1), 1, woven)
                wg_q = quantise(f"wg{b}", woven, PASS)
                z_q.append(quantise(f"z{b - 1}", z, M, slot=raw_slot(b, 1)))
            first_stage(ww_q[b], 2, receivers, wanted)
            first_stage(ww_q[b], 3, receivers, wanted)
            for t in range(PACK):
                first_stage(wg_q, t, senders, given)

        WIDE = M // 2

        def second_stage(a, u, z_codes, z_scale):
            for g in range(N // P):
                nc.tensor.matmul_mx(
                    out=banks[4 * u + 2 * g][:, 0:WIDE],
                    lhsT=w3_q[a][0][:, P * g : P * (g + 1)].bitcast(E4M3),
                    lhsT_scale=w3_q[a][1][:, P * g : P * (g + 1)],
                    rhs=z_codes.bitcast(E4M3),
                    rhs_scale=z_scale,
                    start=(a == 0),
                    stop=(a == BLOCKS - 1),
                )
                for c in range(WIDE // P):
                    nc.tensor.matmul_mx(
                        out=banks[4 * u + 2 * g + 1][:, P * c : P * (c + 1)],
                        lhsT=w4_codes[:, a, 2 * P * g : 2 * P * (g + 1)].bitcast(E2M1),
                        lhsT_scale=w4_scale[:, a, P * g : P * (g + 1)],
                        rhs=z_codes[:, P * c : P * (c + 1)].bitcast(E4M3),
                        rhs_scale=z_scale[:, P * c : P * (c + 1)],
                        start=(a == 0 and c == 0),
                        stop=(a == BLOCKS - 1 and c == WIDE // P - 1),
                    )

        def gate(u, g):
            gated = picked.tile([P, WIDE], F32, name=f"gated{u}_{g}")
            nc.scalar.activation(
                out=gated[:],
                in_=banks[4 * u + 2 * g][:, 0:WIDE],
                func=mybir.ActivationFunctionType.Silu,
                bias=bias[:, g : g + 1],
            )
            return gated

        def finish(u, g, gated):
            score = picked.tile([P, WIDE], F32, name=f"score{u}_{g}")
            nc.vector.tensor_tensor(
                out=score[:], in0=banks[4 * u + 2 * g + 1][:, 0:WIDE], in1=gated[:], op=mybir.AluOpType.add
            )
            nc.sync.dma_start(out=out[P * g : P * (g + 1), WIDE * u : WIDE * (u + 1)], in_=score[:])

        last = BLOCKS - 1
        z_last = []
        for a in range(BLOCKS):
            w3_q.append(quantise(f"w3{a}", weave_w3(a), N))
            if a < last:
                cut = slice(WIDE * a, WIDE * (a + 1))
                z = rows.tile([P, PACK * WIDE], BF16, name="z_last", tag=f"row{2 + a}", align_bytes=64)
                meet(z, given[:, :, cut], wanted[:, :, cut])
                z_last.append(z)
                for u in range(2):
                    cut = slice(WIDE * u, WIDE * (u + 1))
                    second_stage(a, u, z_q[a][0][:, cut], z_q[a][1][:, cut])
        for u in range(2):
            codes, scale = quantise(f"z_last{u}", z_last[u], WIDE)
            second_stage(last, u, codes[:], scale[:])
        for u in range(2):
            for g in range(N // P):
                finish(u, g, gate(u, g))
